import numpy as np
import ml_dtypes


def mxq(x, axis, fmt="e4m3"):
    dtype, down = {"e4m3": (ml_dtypes.float8_e4m3fn, 7), "e5m2": (ml_dtypes.float8_e5m2, 14)}[fmt]
    v = np.moveaxis(np.asarray(x, np.float32).astype(ml_dtypes.bfloat16).astype(np.float64), axis, -1)
    blocks = v.reshape(v.shape[:-1] + (-1, 32))
    amax = np.abs(blocks).max(-1, keepdims=True)
    byte = np.maximum(np.where(amax > 0, np.frexp(amax)[1] - 1 + 127, 0) - down, 1)
    scale = np.exp2(byte - 127.0)
    codes = (blocks / scale).astype(np.float32).astype(dtype).astype(np.float64)
    return np.moveaxis((codes * scale).reshape(v.shape), -1, axis)


WIDE = False


def mx_kscale(k):
    if not WIDE:
        return np.ones(k)
    levels = np.array([10, -10, 5, -5, 0])
    if k % 512:
        return np.exp2(np.random.permutation(np.resize(levels, k // 32))).repeat(32)
    a = np.empty((k // 512, 16))
    for p in range(k // 512):
        a[p, :8] = np.random.permutation(np.resize(levels, 8))
        for g in range(8):
            far = levels[np.abs(levels - a[p, g]) >= 10]
            a[p, g + 8] = far[np.random.randint(len(far))]
    return np.exp2(a.ravel()).repeat(32)


def f64(x):
    return np.asarray(x).astype(np.float64)


def striped(idx):
    return np.tile(idx.reshape(-1, 16).T, (8, 1)).astype(np.uint16)


def unstriped(offs):
    return offs[:16].T.reshape(-1).astype(np.int64)


def striped8(idx):
    return np.concatenate([x.reshape(-1, 16).T for x in idx]).astype(np.uint16)


def runs(offs, k):
    lists = np.stack([offs[16 * r : 16 * r + 16].T.reshape(-1) for r in range(8)]).astype(np.int64)
    return lists[np.arange(k) % 512 // 64]


def pack_weight(w):
    k, n = w.shape
    w = f64(np.asarray(w, np.float32).astype(ml_dtypes.bfloat16)).reshape(k // 32, 32, n)
    amax = np.abs(w).max(1)
    byte = np.clip(np.where(amax > 0, np.frexp(amax)[1] - 1 + 127 - 7, 1), 1, 254)
    scaled = (w * np.exp2(127.0 - byte)[:, None, :]).reshape(k, n).astype(np.float32)
    words = np.ascontiguousarray(scaled.reshape(k // 512, 128, 4, n).transpose(0, 1, 3, 2)).astype(ml_dtypes.float8_e4m3fn).view(np.uint8)
    return words, np.ascontiguousarray(byte.astype(np.uint8).reshape(k // 512, 16, n))


def unpack_weight(words, scales):
    g, p, n, _ = words.shape
    vals = np.ascontiguousarray(words).view(ml_dtypes.float8_e4m3fn).astype(np.float64) * np.repeat(np.exp2(scales.astype(np.float64) - 127.0), 8, axis=1)[..., None]
    return vals.transpose(0, 1, 3, 2).reshape(g * 512, n)

def planes(y):
    n, m = y.shape
    v = y.astype(np.float32).astype(ml_dtypes.bfloat16).astype(np.float64).reshape(n // 32, 32, m)
    top = np.abs(v).max(1)
    byte = np.clip(np.where(top > 0, np.frexp(top)[1] - 1 + 127 - 7, 1), 1, 254)
    codes = (v * np.exp2(127.0 - byte)[:, None, :]).reshape(n, m).astype(np.float32).astype(ml_dtypes.float8_e4m3fn).view(np.uint8)
    words = codes.reshape(n // 512, 128, 4, m).transpose(0, 1, 3, 2)
    return np.ascontiguousarray(words), np.ascontiguousarray(byte.astype(np.uint8).reshape(n // 512, 16, m))


K, T, S, V, H, C = 512, 2048, 512, 256, 512, 512


def setup_inputs():
    n = np.random.standard_normal
    s = mx_kscale(K)[:, None]
    packed_xT = pack_weight(n((K, T)) * s)
    packed_w1 = pack_weight(n((K, H)) / np.sqrt(K) / s)
    return {
        "x_words": packed_xT[0],
        "x_scales": packed_xT[1],
        "w1_words": packed_w1[0],
        "w1_scales": packed_w1[1],
        "gs": (np.random.uniform(0.5, 1.5, (K, 1)) / s).astype(np.float32),
        "offs": striped(np.random.permutation(T)[:S]),
        "i_l": striped8(np.stack([np.random.permutation(S)[:V] for _ in range(8)])),
        "k_l": striped8(np.stack([np.random.permutation(S)[:V] for _ in range(8)])),
        "j_l": striped8(np.stack([np.random.permutation(S)[:V] for _ in range(8)])),
        "cand": striped(np.random.permutation(T)[:C]),
    }


def reference(x_words, x_scales, w1_words, w1_scales, gs, offs, i_l, k_l, j_l, cand):
    x_cand = unpack_weight(x_words, x_scales)[:, unstriped(cand)]
    xq = unpack_weight(x_words, x_scales)[:, unstriped(offs)]
    y = unpack_weight(w1_words, w1_scales).T @ xq
    a = y[np.arange(H)[:, None], runs(i_l, H)] - (y[np.arange(H)[:, None], runs(k_l, H)])
    b = y[np.arange(H)[:, None], runs(j_l, H)] - (y[np.arange(H)[:, None], runs(k_l, H)])
    z = f64(gs) * ((a * b) / (np.sqrt(((a) ** 2 + 0.25) * ((b) ** 2 + 0.25))))
    out_0 = 0.0625 * ((x_cand.T @ mxq(z, 0, "e4m3")))
    return (out_0,) + planes(out_0)

@@ -1,0 +1,199 @@
+from contextlib import ExitStack
+
+import concourse.mybir as mybir
+
+K, T, S, V, H, C = 512, 2048, 512, 256, 512, 512
+FLOPS = 2 * K * H * S + 2 * K * C * V
+
+F32 = mybir.dt.float32
+BF16 = mybir.dt.bfloat16
+I32 = mybir.dt.int32
+U32 = mybir.dt.uint32
+U16 = mybir.dt.uint16
+U8 = mybir.dt.uint8
+FP8X4 = mybir.dt.float8_e4m3fn_x4
+ACT = mybir.ActivationFunctionType
+ALU = mybir.AluOpType
+
+P = 128
+PACK = 4
+HALF = V // 2
+
+
+def as_words(dram):
+    return dram[0].rearrange("p n t -> p (n t)").bitcast(I32)
+
+
+def load_scale_rows(queue, plane, scales):
+    rows = scales[0].bitcast(I32)
+    view = plane[:].bitcast(I32)
+    for q in range(4):
+        queue.dma_start(out=view[32 * q : 32 * q + 4, :], in_=rows[4 * q : 4 * q + 4, :])
+
+
+def deal(engine, dealt, plain, run):
+    engine.tensor_copy(
+        out=dealt.rearrange("p (t c i) -> p c t i", t=PACK, i=run),
+        in_=plain.rearrange("p (c i t) -> p c t i", t=PACK, i=run),
+    )
+
+
+def woven(tile):
+    return tile.rearrange("p (c i t) -> p c t i", t=PACK, i=4)
+
+
+def planar(tile):
+    return tile.rearrange("p t (c i) -> p c t i", i=4)
+
+
+def tile_picked_bondang_none_po_kernel(
+    tc, x_words, x_scales, w1_words, w1_scales, gs, offs, i_l, k_l, j_l, cand, out_0, out_1, out_2
+):
+    nc = tc.nc
+    with ExitStack() as ctx:
+        lists = ctx.enter_context(tc.tile_pool(name="lists", bufs=1))
+        keep = ctx.enter_context(tc.tile_pool(name="keep", bufs=1))
+        psum = ctx.enter_context(tc.psum_pool(name="psum", bufs=1))
+
+        offs_t = lists.tile([P, S // 16], U16, name="offs_t")
+        cand_t = lists.tile([P, C // 16], U16, name="cand_t")
+        k_t = lists.tile([P, V // 16], U16, name="k_t")
+        i_t = lists.tile([P, V // 16], U16, name="i_t")
+        j_t = lists.tile([P, V // 16], U16, name="j_t")
+
+        def sb(name, shape, dtype, tag=None):
+            return keep.tile(shape, dtype, name=name, tag=tag or name, align_bytes=64)
+
+        xs = sb("xs", [P, T], U8)
+        xw = sb("xw", [P, T], U32)
+        ws = sb("ws", [P, H], U8, "ws_then_cw")
+        ww = sb("ww", [P, H], U32)
+        gs_t = sb("gs_t", [P, PACK], F32)
+        quarter = sb("quarter", [P, 1], F32)
+        warm = sb("warm", [P, 1], F32)
+
+        nc.vector.memset(xs[:].bitcast(I32), 0)
+        nc.gpsimd.memset(quarter[:], 0.25)
+        nc.vector.memset(ws[:].bitcast(I32), 0)
+        nc.scalar.activation(out=warm[:], in_=quarter[:], func=ACT.Abs_reciprocal_sqrt, bias=quarter[:])
+
+        nc.sync.dma_start(offs_t[:], offs)
+        nc.sync.dma_start(cand_t[:], cand)
+        load_scale_rows(nc.sync, xs, x_scales)
+        nc.sync.dma_start(out=ww[:].bitcast(I32), in_=as_words(w1_words))
+        nc.sync.dma_start(out=xw[:].bitcast(I32), in_=as_words(x_words))
+        load_scale_rows(nc.sync, ws, w1_scales)
+        nc.sync.dma_start(k_t[:], k_l)
+        nc.sync.dma_start(i_t[:], i_l)
+        nc.sync.dma_start(j_t[:], j_l)
+        nc.sync.dma_start(out=gs_t[:], in_=gs.rearrange("(p t) o -> p (t o)", t=PACK))
+
+        qs = sb("qs", [P, S], U8)
+        qw = sb("qw", [P, S], U32)
+        cs = sb("cs", [P, C], U8)
+        cw = sb("cw", [P, C], U32, "ws_then_cw")
+        csd = sb("csd", [P, C], U8)
+        cwd = sb("cwd", [P, C], U32)
+        wsd = sb("wsd", [P, H], U8)
+        wwd = sb("wwd", [P, H], U32)
+
+        nc.vector.tensor_copy(out=qs[:], in_=xs[:].indirect(offs_t[:]))
+        nc.vector.tensor_copy(out=cs[:], in_=xs[:].indirect(cand_t[:]))
+        deal(nc.vector, wwd[:].bitcast(I32), ww[:].bitcast(I32), 4)
+        deal(nc.vector, wsd[:], ws[:], 16)
+        nc.vector.tensor_copy(out=qw[:], in_=xw[:].indirect(offs_t[:]))
+        deal(nc.vector, csd[:], cs[:], 16)
+        nc.vector.tensor_copy(out=cw[:], in_=xw[:].indirect(cand_t[:]))
+        deal(nc.vector, cwd[:].bitcast(I32), cw[:].bitcast(I32), 4)
+
+        y = []
+        for t in range(PACK):
+            cols = slice(t * P, (t + 1) * P)
+            acc = psum.tile([P, S], F32, name=f"y_acc{t}")
+            nc.tensor.matmul_mx(
+                out=acc[:], lhsT=wwd[:, cols].bitcast(FP8X4), lhsT_scale=wsd[:, cols],
+                rhs=qw[:].bitcast(FP8X4), rhs_scale=qs[:], start=True, stop=True,
+            )
+            y_t = sb(f"y{t}", [P, S], F32)
+            nc.scalar.copy(out=y_t[:], in_=acc[:])
+            y.append(y_t)
+
+        num = sb("num", [P, 2, PACK, HALF], F32)
+        inv = sb("inv", [P, 2, PACK, HALF], F32)
+
+        def fetch(t, h0, h1):
+            n = (h1 - h0) * HALF
+            cols = slice(h0 * HALF // 16, h1 * HALF // 16)
+            tip = sb(f"tip{t}_{h0}", [P, n], F32)
+            ab = sb(f"ab{t}_{h0}", [P, 2, n], F32)
+            nc.vector.tensor_copy(out=tip[:], in_=y[t][:].indirect(k_t[:, cols]))
+            nc.vector.tensor_tensor(out=ab[:, 0, :], in0=y[t][:].indirect(i_t[:, cols]), in1=tip[:], op=ALU.subtract)
+            nc.vector.tensor_tensor(out=ab[:, 1, :], in0=y[t][:].indirect(j_t[:, cols]), in1=tip[:], op=ALU.subtract)
+            sq = sb(f"sq{t}_{h0}", [P, 2, n], F32)
+            root = sb(f"root{t}_{h0}", [P, 2, n], F32)
+            nc.scalar.activation(out=sq[:], in_=ab[:], func=ACT.Square)
+            nc.scalar.activation(out=root[:], in_=sq[:], func=ACT.Abs_reciprocal_sqrt, bias=quarter[:])
+            return ab, root
+
+        def combine(t, h0, h1, ab, root):
+            def halves(ap):
+                return ap.rearrange("p (h v) -> p h v", v=HALF)
+
+            nc.vector.scalar_tensor_tensor(
+                out=num[:, h0:h1, t, :], in0=halves(ab[:, 0, :]), scalar=gs_t[:, t : t + 1],
+                in1=halves(ab[:, 1, :]), op0=ALU.mult, op1=ALU.mult,
+            )
+            nc.vector.tensor_tensor(
+                out=inv[:, h0:h1, t, :], in0=halves(root[:, 0, :]), in1=halves(root[:, 1, :]), op=ALU.mult
+            )
+
+        pieces = [(0, 0, 2), (1, 0, 2), (2, 0, 2), (3, 0, 1), (3, 1, 2)]
+        made = []
+        for n, piece in enumerate(pieces):
+            made.append(fetch(*piece))
+            if n > 0:
+                combine(*pieces[n - 1], *made[n - 1])
+
+        ow = sb("ow", [P, V], U32)
+        osc = sb("osc", [P, V], U8)
+        out_rows = out_0.rearrange("(p t) v -> p t v", t=PACK)
+
+        def quantise_z(h):
+            zb = sb(f"zb{h}", [P, PACK * HALF], BF16)
+            zw = sb(f"zw{h}", [P, HALF], U32)
+            zs = sb(f"zs{h}", [P, HALF], U8)
+            nc.vector.tensor_tensor(out=woven(zb[:]), in0=planar(num[:, h]), in1=planar(inv[:, h]), op=ALU.mult)
+            nc.vector.quantize_mx(out=zw[:].bitcast(FP8X4), scales=zs[:], in_=zb[:])
+            return zw, zs
+
+        def score(h, zw, zs):
+            v_cols = slice(h * HALF, (h + 1) * HALF)
+            acc = psum.tile([P, PACK, HALF], F32, name=f"o_acc{h}")
+            for t in range(PACK):
+                cols = slice(t * P, (t + 1) * P)
+                nc.tensor.matmul_mx(
+                    out=acc[:, t, :], lhsT=cwd[:, cols].bitcast(FP8X4), lhsT_scale=csd[:, cols],
+                    rhs=zw[:].bitcast(FP8X4), rhs_scale=zs[:], start=True, stop=True,
+                )
+            res = sb(f"res{h}", [P, PACK, HALF], F32)
+            ob = sb(f"ob{h}", [P, PACK * HALF], BF16)
+            nc.scalar.activation(out=res[:], in_=acc[:], func=ACT.Copy, scale=0.0625)
+            nc.sync.dma_start(out=out_rows[:, :, v_cols], in_=res[:])
+            if h == 0:
+                nc.scalar.copy(out=woven(ob[:]), in_=planar(res[:]))
+            else:
+                nc.vector.tensor_copy(out=woven(ob[:]), in_=planar(res[:]))
+            nc.vector.quantize_mx(out=ow[:, v_cols].bitcast(FP8X4), scales=osc[:, v_cols], in_=ob[:])
+            nc.sync.dma_start(out=as_words(out_1)[:, v_cols], in_=ow[:, v_cols].bitcast(I32))
+
+        z0 = quantise_z(0)
+        combine(*pieces[-1], *made[-1])
+        z1 = quantise_z(1)
+        score(0, *z0)
+        score(1, *z1)
+
+        rows = out_2[0].bitcast(I32)
+        view = osc[:].bitcast(I32)
+        for q in range(4):
+            queue = nc.scalar if q % 2 == 0 else nc.sync
+            queue.dma_start(out=rows[4 * q : 4 * q + 4, :], in_=view[32 * q : 32 * q + 4, :])

@@ -1,6 +1,7 @@
 from contextlib import ExitStack
 
 import concourse.mybir as mybir
+from concourse.masks import make_identity
 
 K, T, S, V, H, C = 512, 2048, 512, 256, 512, 512
 FLOPS = 2 * K * H * S + 2 * K * C * V
@@ -18,6 +19,7 @@ ALU = mybir.AluOpType
 P = 128
 PACK = 4
 HALF = V // 2
+TURNED = (0,)
 
 
 def as_words(dram):
@@ -39,11 +41,11 @@ def deal(engine, dealt, plain, run):
 
 
 def woven(tile):
-    return tile.rearrange("p (c i t) -> p c t i", t=PACK, i=4)
+    return tile.rearrange("p (c i t) -> p c t i", t=PACK, i=2)
 
 
 def planar(tile):
-    return tile.rearrange("p t (c i) -> p c t i", i=4)
+    return tile.rearrange("p t (c i) -> p c t i", i=2)
 
 
 def tile_picked_bondang_none_po_kernel(
@@ -70,17 +72,22 @@ def tile_picked_bondang_none_po_kernel(
         ww = sb("ww", [P, H], U32)
         gs_t = sb("gs_t", [P, PACK], F32)
         quarter = sb("quarter", [P, 1], F32)
+        less_quarter = sb("less_quarter", [P, 1], F32)
+        ident = sb("ident", [P, P], F32)
         warm = sb("warm", [P, 1], F32)
 
         nc.vector.memset(xs[:].bitcast(I32), 0)
-        nc.gpsimd.memset(quarter[:], 0.25)
+        nc.vector.memset(quarter[:], 0.25)
         nc.vector.memset(ws[:].bitcast(I32), 0)
+        nc.vector.memset(less_quarter[:], -0.25)
+        nc.vector.memset(ident[:], 0.0)
+        make_identity(nc, ident[:], nomemset=True)
         nc.scalar.activation(out=warm[:], in_=quarter[:], func=ACT.Abs_reciprocal_sqrt, bias=quarter[:])
 
-        nc.sync.dma_start(offs_t[:], offs)
-        nc.sync.dma_start(cand_t[:], cand)
         load_scale_rows(nc.sync, xs, x_scales)
         nc.sync.dma_start(out=ww[:].bitcast(I32), in_=as_words(w1_words))
+        nc.sync.dma_start(offs_t[:], offs)
+        nc.sync.dma_start(cand_t[:], cand)
         nc.sync.dma_start(out=xw[:].bitcast(I32), in_=as_words(x_words))
         load_scale_rows(nc.sync, ws, w1_scales)
         nc.sync.dma_start(k_t[:], k_l)
@@ -91,54 +98,94 @@ def tile_picked_bondang_none_po_kernel(
         qs = sb("qs", [P, S], U8)
         qw = sb("qw", [P, S], U32)
         cs = sb("cs", [P, C], U8)
-        cw = sb("cw", [P, C], U32, "ws_then_cw")
         csd = sb("csd", [P, C], U8)
-        cwd = sb("cwd", [P, C], U32)
+        cwd = sb("cwd", [P, C], U32, "ws_then_cw")
         wsd = sb("wsd", [P, H], U8)
         wwd = sb("wwd", [P, H], U32)
 
         nc.vector.tensor_copy(out=qs[:], in_=xs[:].indirect(offs_t[:]))
         nc.vector.tensor_copy(out=cs[:], in_=xs[:].indirect(cand_t[:]))
         deal(nc.vector, wwd[:].bitcast(I32), ww[:].bitcast(I32), 4)
-        deal(nc.vector, wsd[:], ws[:], 16)
-        nc.vector.tensor_copy(out=qw[:], in_=xw[:].indirect(offs_t[:]))
+        for part in range(2):
+            nc.vector.tensor_copy(
+                out=qw[:, part * S // 2 : (part + 1) * S // 2],
+                in_=xw[:].indirect(offs_t[:, part * S // 32 : (part + 1) * S // 32]),
+            )
+            if part == 0:
+                deal(nc.vector, wsd[:], ws[:], 16)
         deal(nc.vector, csd[:], cs[:], 16)
-        nc.vector.tensor_copy(out=cw[:], in_=xw[:].indirect(cand_t[:]))
-        deal(nc.vector, cwd[:].bitcast(I32), cw[:].bitcast(I32), 4)
+        nc.vector.tensor_copy(out=cwd[:].rearrange("p (t m) -> p m t", t=PACK), in_=xw[:].indirect(cand_t[:]))
 
         y = []
         for t in range(PACK):
             cols = slice(t * P, (t + 1) * P)
-            acc = psum.tile([P, S], F32, name=f"y_acc{t}")
-            nc.tensor.matmul_mx(
-                out=acc[:], lhsT=wwd[:, cols].bitcast(FP8X4), lhsT_scale=wsd[:, cols],
-                rhs=qw[:].bitcast(FP8X4), rhs_scale=qs[:], start=True, stop=True,
-            )
             y_t = sb(f"y{t}", [P, S], F32)
-            nc.scalar.copy(out=y_t[:], in_=acc[:])
+            width = S // 2 if t == 0 else S
+            for s0 in range(0, S, width):
+                atoms = slice(s0, s0 + width)
+                acc = psum.tile([P, width], F32, name=f"y_acc{t}_{s0}", tag=f"bank{t}" if s0 == 0 else "bank4")
+                nc.tensor.matmul_mx(
+                    out=acc[:], lhsT=wwd[:, cols].bitcast(FP8X4), lhsT_scale=wsd[:, cols],
+                    rhs=qw[:, atoms].bitcast(FP8X4), rhs_scale=qs[:, atoms], start=True, stop=True,
+                )
+                nc.scalar.copy(out=y_t[:, atoms], in_=acc[:])
             y.append(y_t)
 
         num = sb("num", [P, 2, PACK, HALF], F32)
         inv = sb("inv", [P, 2, PACK, HALF], F32)
 
-        def fetch(t, h0, h1):
+        def fetch_tip(t, h0, h1):
+            cols = slice(h0 * HALF // 16, h1 * HALF // 16)
+            tip = sb(f"tip{t}_{h0}", [P, (h1 - h0) * HALF], F32)
+            nc.vector.tensor_copy(out=tip[:], in_=y[t][:].indirect(k_t[:, cols]))
+            return tip
+
+        def fetch(t, h0, h1, tip):
             n = (h1 - h0) * HALF
             cols = slice(h0 * HALF // 16, h1 * HALF // 16)
-            tip = sb(f"tip{t}_{h0}", [P, n], F32)
             ab = sb(f"ab{t}_{h0}", [P, 2, n], F32)
-            nc.vector.tensor_copy(out=tip[:], in_=y[t][:].indirect(k_t[:, cols]))
             nc.vector.tensor_tensor(out=ab[:, 0, :], in0=y[t][:].indirect(i_t[:, cols]), in1=tip[:], op=ALU.subtract)
             nc.vector.tensor_tensor(out=ab[:, 1, :], in0=y[t][:].indirect(j_t[:, cols]), in1=tip[:], op=ALU.subtract)
-            sq = sb(f"sq{t}_{h0}", [P, 2, n], F32)
-            root = sb(f"root{t}_{h0}", [P, 2, n], F32)
-            nc.scalar.activation(out=sq[:], in_=ab[:], func=ACT.Square)
-            nc.scalar.activation(out=root[:], in_=sq[:], func=ACT.Abs_reciprocal_sqrt, bias=quarter[:])
-            return ab, root
+            return ab
 
-        def combine(t, h0, h1, ab, root):
+        def turn(out, parts):
+            for n, part in enumerate(parts):
+                nc.tensor.matmul(
+                    out=out, lhsT=part, rhs=ident[:], is_transpose=True, start=n == 0, stop=n == len(parts) - 1
+                )
+
+        def combine_turned(t, ab):
+            prod = sb(f"prod{t}", [P, 2, HALF], F32)
+            nc.vector.tensor_tensor(
+                out=prod[:].rearrange("p h v -> p (h v)"), in0=ab[:, 0, :], in1=ab[:, 1, :], op=ALU.mult
+            )
+            there = psum.tile([P, 2, 2, P], F32, name=f"there{t}", tag=f"bank{t}")
+            back = psum.tile([P, 2, HALF], F32, name=f"back{t}", tag=f"back{t % 2}")
+            terms = sb(f"terms{t}", [P, 2, 2, P], F32)
+            for h in range(2):
+                v_cols = slice(h * HALF, (h + 1) * HALF)
+                turn(there[:, 0, h, :], [ab[:, 0, v_cols], ab[:, 1, v_cols]])
+            for h in range(2):
+                turn(there[:, 1, h, :], [prod[:, h, :]])
+            nc.scalar.activation(out=terms[:, 0], in_=there[:, 0], func=ACT.Square, scale=0.5)
+            nc.scalar.activation(out=terms[:, 1], in_=there[:, 1], func=ACT.Square, bias=less_quarter[:])
+            for h in range(2):
+                turn(back[:, h, :], [terms[:, 0, h, :], terms[:, 1, h, :]])
+            nc.scalar.activation(out=num[:, :, t, :], in_=prod[:], func=ACT.Copy, scale=gs_t[:, t : t + 1])
+            nc.scalar.activation(out=inv[:, :, t, :], in_=back[:], func=ACT.Abs_reciprocal_sqrt)
+
+        def combine(t, h0, h1, ab):
             def halves(ap):
                 return ap.rearrange("p (h v) -> p h v", v=HALF)
 
+            if t in TURNED:
+                combine_turned(t, ab)
+                return
+            n = (h1 - h0) * HALF
+            sq = sb(f"sq{t}_{h0}", [P, 2, n], F32, f"sq{t}")
+            root = sb(f"root{t}_{h0}", [P, 2, n], F32)
+            nc.scalar.activation(out=sq[:], in_=ab[:], func=ACT.Square)
+            nc.scalar.activation(out=root[:], in_=sq[:], func=ACT.Abs_reciprocal_sqrt, bias=quarter[:])
             nc.vector.scalar_tensor_tensor(
                 out=num[:, h0:h1, t, :], in0=halves(ab[:, 0, :]), scalar=gs_t[:, t : t + 1],
                 in1=halves(ab[:, 1, :]), op0=ALU.mult, op1=ALU.mult,
@@ -149,10 +196,13 @@ def tile_picked_bondang_none_po_kernel(
 
         pieces = [(0, 0, 2), (1, 0, 2), (2, 0, 2), (3, 0, 1), (3, 1, 2)]
         made = []
+        tips = [fetch_tip(*pieces[0])]
         for n, piece in enumerate(pieces):
-            made.append(fetch(*piece))
-            if n > 0:
-                combine(*pieces[n - 1], *made[n - 1])
+            if n + 1 < len(pieces):
+                tips.append(fetch_tip(*pieces[n + 1]))
+            made.append(fetch(*piece, tips[n]))
+            if n + 1 < len(pieces):
+                combine(*piece, made[n])
 
         ow = sb("ow", [P, V], U32)
         osc = sb("osc", [P, V], U8)
@@ -168,26 +218,24 @@ def tile_picked_bondang_none_po_kernel(
 
         def score(h, zw, zs):
             v_cols = slice(h * HALF, (h + 1) * HALF)
-            acc = psum.tile([P, PACK, HALF], F32, name=f"o_acc{h}")
-            for t in range(PACK):
-                cols = slice(t * P, (t + 1) * P)
-                nc.tensor.matmul_mx(
-                    out=acc[:, t, :], lhsT=cwd[:, cols].bitcast(FP8X4), lhsT_scale=csd[:, cols],
-                    rhs=zw[:].bitcast(FP8X4), rhs_scale=zs[:], start=True, stop=True,
-                )
             res = sb(f"res{h}", [P, PACK, HALF], F32)
             ob = sb(f"ob{h}", [P, PACK * HALF], BF16)
-            nc.scalar.activation(out=res[:], in_=acc[:], func=ACT.Copy, scale=0.0625)
+            for pair in range(2):
+                acc = psum.tile([P, 2, HALF], F32, name=f"o_acc{h}{pair}", tag=f"bank{2 * h + pair}")
+                for e in range(2):
+                    cols = slice((2 * pair + e) * P, (2 * pair + e + 1) * P)
+                    nc.tensor.matmul_mx(
+                        out=acc[:, e, :], lhsT=cwd[:, cols].bitcast(FP8X4), lhsT_scale=csd[:, cols],
+                        rhs=zw[:].bitcast(FP8X4), rhs_scale=zs[:], start=True, stop=True,
+                    )
+                nc.scalar.activation(out=res[:, 2 * pair : 2 * pair + 2, :], in_=acc[:], func=ACT.Copy, scale=0.0625)
             nc.sync.dma_start(out=out_rows[:, :, v_cols], in_=res[:])
-            if h == 0:
-                nc.scalar.copy(out=woven(ob[:]), in_=planar(res[:]))
-            else:
-                nc.vector.tensor_copy(out=woven(ob[:]), in_=planar(res[:]))
+            nc.vector.tensor_copy(out=woven(ob[:]), in_=planar(res[:]))
             nc.vector.quantize_mx(out=ow[:, v_cols].bitcast(FP8X4), scales=osc[:, v_cols], in_=ob[:])
             nc.sync.dma_start(out=as_words(out_1)[:, v_cols], in_=ow[:, v_cols].bitcast(I32))
 
         z0 = quantise_z(0)
-        combine(*pieces[-1], *made[-1])
+        combine(*pieces[-1], made[-1])
         z1 = quantise_z(1)
         score(0, *z0)
         score(1, *z1)

from contextlib import ExitStack

import concourse.mybir as mybir
from concourse.masks import make_identity

K, T, S, V, H, C = 512, 2048, 512, 256, 512, 512
FLOPS = 2 * K * H * S + 2 * K * C * V

F32 = mybir.dt.float32
BF16 = mybir.dt.bfloat16
I32 = mybir.dt.int32
U32 = mybir.dt.uint32
U16 = mybir.dt.uint16
U8 = mybir.dt.uint8
FP8X4 = mybir.dt.float8_e4m3fn_x4
ACT = mybir.ActivationFunctionType
ALU = mybir.AluOpType

P = 128
PACK = 4
HALF = V // 2
TURNED = (0,)


def as_words(dram):
    return dram[0].rearrange("p n t -> p (n t)").bitcast(I32)


def load_scale_rows(queue, plane, scales):
    rows = scales[0].bitcast(I32)
    view = plane[:].bitcast(I32)
    for q in range(4):
        queue.dma_start(out=view[32 * q : 32 * q + 4, :], in_=rows[4 * q : 4 * q + 4, :])


def deal(engine, dealt, plain, run):
    engine.tensor_copy(
        out=dealt.rearrange("p (t c i) -> p c t i", t=PACK, i=run),
        in_=plain.rearrange("p (c i t) -> p c t i", t=PACK, i=run),
    )


def woven(tile):
    return tile.rearrange("p (c i t) -> p c t i", t=PACK, i=2)


def planar(tile):
    return tile.rearrange("p t (c i) -> p c t i", i=2)


def tile_picked_bondang_none_po_kernel(
    tc, x_words, x_scales, w1_words, w1_scales, gs, offs, i_l, k_l, j_l, cand, out_0, out_1, out_2
):
    nc = tc.nc
    with ExitStack() as ctx:
        lists = ctx.enter_context(tc.tile_pool(name="lists", bufs=1))
        keep = ctx.enter_context(tc.tile_pool(name="keep", bufs=1))
        psum = ctx.enter_context(tc.psum_pool(name="psum", bufs=1))

        offs_t = lists.tile([P, S // 16], U16, name="offs_t")
        cand_t = lists.tile([P, C // 16], U16, name="cand_t")
        k_t = lists.tile([P, V // 16], U16, name="k_t")
        i_t = lists.tile([P, V // 16], U16, name="i_t")
        j_t = lists.tile([P, V // 16], U16, name="j_t")

        def sb(name, shape, dtype, tag=None):
            return keep.tile(shape, dtype, name=name, tag=tag or name, align_bytes=64)

        xs = sb("xs", [P, T], U8)
        xw = sb("xw", [P, T], U32)
        ws = sb("ws", [P, H], U8, "ws_then_cw")
        ww = sb("ww", [P, H], U32)
        gs_t = sb("gs_t", [P, PACK], F32)
        quarter = sb("quarter", [P, 1], F32)
        less_quarter = sb("less_quarter", [P, 1], F32)
        ident = sb("ident", [P, P], F32)
        warm = sb("warm", [P, 1], F32)

        nc.vector.memset(xs[:].bitcast(I32), 0)
        nc.vector.memset(quarter[:], 0.25)
        nc.vector.memset(ws[:].bitcast(I32), 0)
        nc.vector.memset(less_quarter[:], -0.25)
        nc.vector.memset(ident[:], 0.0)
        make_identity(nc, ident[:], nomemset=True)
        nc.scalar.activation(out=warm[:], in_=quarter[:], func=ACT.Abs_reciprocal_sqrt, bias=quarter[:])

        load_scale_rows(nc.sync, xs, x_scales)
        nc.sync.dma_start(out=ww[:].bitcast(I32), in_=as_words(w1_words))
        nc.sync.dma_start(offs_t[:], offs)
        nc.sync.dma_start(cand_t[:], cand)
        nc.sync.dma_start(out=xw[:].bitcast(I32), in_=as_words(x_words))
        load_scale_rows(nc.sync, ws, w1_scales)
        nc.sync.dma_start(k_t[:], k_l)
        nc.sync.dma_start(i_t[:], i_l)
        nc.sync.dma_start(j_t[:], j_l)
        nc.sync.dma_start(out=gs_t[:], in_=gs.rearrange("(p t) o -> p (t o)", t=PACK))

        qs = sb("qs", [P, S], U8)
        qw = sb("qw", [P, S], U32)
        cs = sb("cs", [P, C], U8)
        csd = sb("csd", [P, C], U8)
        cwd = sb("cwd", [P, C], U32, "ws_then_cw")
        wsd = sb("wsd", [P, H], U8)
        wwd = sb("wwd", [P, H], U32)

        nc.vector.tensor_copy(out=qs[:], in_=xs[:].indirect(offs_t[:]))
        nc.vector.tensor_copy(out=cs[:], in_=xs[:].indirect(cand_t[:]))
        deal(nc.vector, wwd[:].bitcast(I32), ww[:].bitcast(I32), 4)
        for part in range(2):
            nc.vector.tensor_copy(
                out=qw[:, part * S // 2 : (part + 1) * S // 2],
                in_=xw[:].indirect(offs_t[:, part * S // 32 : (part + 1) * S // 32]),
            )
            if part == 0:
                deal(nc.vector, wsd[:], ws[:], 16)
        deal(nc.vector, csd[:], cs[:], 16)
        nc.vector.tensor_copy(out=cwd[:].rearrange("p (t m) -> p m t", t=PACK), in_=xw[:].indirect(cand_t[:]))

        y = []
        for t in range(PACK):
            cols = slice(t * P, (t + 1) * P)
            y_t = sb(f"y{t}", [P, S], F32)
            width = S // 2 if t == 0 else S
            for s0 in range(0, S, width):
                atoms = slice(s0, s0 + width)
                acc = psum.tile([P, width], F32, name=f"y_acc{t}_{s0}", tag=f"bank{t}" if s0 == 0 else "bank4")
                nc.tensor.matmul_mx(
                    out=acc[:], lhsT=wwd[:, cols].bitcast(FP8X4), lhsT_scale=wsd[:, cols],
                    rhs=qw[:, atoms].bitcast(FP8X4), rhs_scale=qs[:, atoms], start=True, stop=True,
                )
                nc.scalar.copy(out=y_t[:, atoms], in_=acc[:])
            y.append(y_t)

        num = sb("num", [P, 2, PACK, HALF], F32)
        inv = sb("inv", [P, 2, PACK, HALF], F32)

        def fetch_tip(t, h0, h1):
            cols = slice(h0 * HALF // 16, h1 * HALF // 16)
            tip = sb(f"tip{t}_{h0}", [P, (h1 - h0) * HALF], F32)
            nc.vector.tensor_copy(out=tip[:], in_=y[t][:].indirect(k_t[:, cols]))
            return tip

        def fetch(t, h0, h1, tip):
            n = (h1 - h0) * HALF
            cols = slice(h0 * HALF // 16, h1 * HALF // 16)
            ab = sb(f"ab{t}_{h0}", [P, 2, n], F32)
            nc.vector.tensor_tensor(out=ab[:, 0, :], in0=y[t][:].indirect(i_t[:, cols]), in1=tip[:], op=ALU.subtract)
            nc.vector.tensor_tensor(out=ab[:, 1, :], in0=y[t][:].indirect(j_t[:, cols]), in1=tip[:], op=ALU.subtract)
            return ab

        def turn(out, parts):
            for n, part in enumerate(parts):
                nc.tensor.matmul(
                    out=out, lhsT=part, rhs=ident[:], is_transpose=True, start=n == 0, stop=n == len(parts) - 1
                )

        def combine_turned(t, ab):
            prod = sb(f"prod{t}", [P, 2, HALF], F32)
            nc.vector.tensor_tensor(
                out=prod[:].rearrange("p h v -> p (h v)"), in0=ab[:, 0, :], in1=ab[:, 1, :], op=ALU.mult
            )
            there = psum.tile([P, 2, 2, P], F32, name=f"there{t}", tag=f"bank{t}")
            back = psum.tile([P, 2, HALF], F32, name=f"back{t}", tag=f"back{t % 2}")
            terms = sb(f"terms{t}", [P, 2, 2, P], F32)
            for h in range(2):
                v_cols = slice(h * HALF, (h + 1) * HALF)
                turn(there[:, 0, h, :], [ab[:, 0, v_cols], ab[:, 1, v_cols]])
            for h in range(2):
                turn(there[:, 1, h, :], [prod[:, h, :]])
            nc.scalar.activation(out=terms[:, 0], in_=there[:, 0], func=ACT.Square, scale=0.5)
            nc.scalar.activation(out=terms[:, 1], in_=there[:, 1], func=ACT.Square, bias=less_quarter[:])
            for h in range(2):
                turn(back[:, h, :], [terms[:, 0, h, :], terms[:, 1, h, :]])
            nc.scalar.activation(out=num[:, :, t, :], in_=prod[:], func=ACT.Copy, scale=gs_t[:, t : t + 1])
            nc.scalar.activation(out=inv[:, :, t, :], in_=back[:], func=ACT.Abs_reciprocal_sqrt)

        def combine(t, h0, h1, ab):
            def halves(ap):
                return ap.rearrange("p (h v) -> p h v", v=HALF)

            if t in TURNED:
                combine_turned(t, ab)
                return
            n = (h1 - h0) * HALF
            sq = sb(f"sq{t}_{h0}", [P, 2, n], F32, f"sq{t}")
            root = sb(f"root{t}_{h0}", [P, 2, n], F32)
            nc.scalar.activation(out=sq[:], in_=ab[:], func=ACT.Square)
            nc.scalar.activation(out=root[:], in_=sq[:], func=ACT.Abs_reciprocal_sqrt, bias=quarter[:])
            nc.vector.scalar_tensor_tensor(
                out=num[:, h0:h1, t, :], in0=halves(ab[:, 0, :]), scalar=gs_t[:, t : t + 1],
                in1=halves(ab[:, 1, :]), op0=ALU.mult, op1=ALU.mult,
            )
            nc.vector.tensor_tensor(
                out=inv[:, h0:h1, t, :], in0=halves(root[:, 0, :]), in1=halves(root[:, 1, :]), op=ALU.mult
            )

        pieces = [(0, 0, 2), (1, 0, 2), (2, 0, 2), (3, 0, 1), (3, 1, 2)]
        made = []
        tips = [fetch_tip(*pieces[0])]
        for n, piece in enumerate(pieces):
            if n + 1 < len(pieces):
                tips.append(fetch_tip(*pieces[n + 1]))
            made.append(fetch(*piece, tips[n]))
            if n + 1 < len(pieces):
                combine(*piece, made[n])

        ow = sb("ow", [P, V], U32)
        osc = sb("osc", [P, V], U8)
        out_rows = out_0.rearrange("(p t) v -> p t v", t=PACK)

        def quantise_z(h):
            zb = sb(f"zb{h}", [P, PACK * HALF], BF16)
            zw = sb(f"zw{h}", [P, HALF], U32)
            zs = sb(f"zs{h}", [P, HALF], U8)
            nc.vector.tensor_tensor(out=woven(zb[:]), in0=planar(num[:, h]), in1=planar(inv[:, h]), op=ALU.mult)
            nc.vector.quantize_mx(out=zw[:].bitcast(FP8X4), scales=zs[:], in_=zb[:])
            return zw, zs

        def score(h, zw, zs):
            v_cols = slice(h * HALF, (h + 1) * HALF)
            res = sb(f"res{h}", [P, PACK, HALF], F32)
            ob = sb(f"ob{h}", [P, PACK * HALF], BF16)
            for pair in range(2):
                acc = psum.tile([P, 2, HALF], F32, name=f"o_acc{h}{pair}", tag=f"bank{2 * h + pair}")
                for e in range(2):
                    cols = slice((2 * pair + e) * P, (2 * pair + e + 1) * P)
                    nc.tensor.matmul_mx(
                        out=acc[:, e, :], lhsT=cwd[:, cols].bitcast(FP8X4), lhsT_scale=csd[:, cols],
                        rhs=zw[:].bitcast(FP8X4), rhs_scale=zs[:], start=True, stop=True,
                    )
                nc.scalar.activation(out=res[:, 2 * pair : 2 * pair + 2, :], in_=acc[:], func=ACT.Copy, scale=0.0625)
            nc.sync.dma_start(out=out_rows[:, :, v_cols], in_=res[:])
            nc.vector.tensor_copy(out=woven(ob[:]), in_=planar(res[:]))
            nc.vector.quantize_mx(out=ow[:, v_cols].bitcast(FP8X4), scales=osc[:, v_cols], in_=ob[:])
            nc.sync.dma_start(out=as_words(out_1)[:, v_cols], in_=ow[:, v_cols].bitcast(I32))

        z0 = quantise_z(0)
        combine(*pieces[-1], made[-1])
        z1 = quantise_z(1)
        score(0, *z0)
        score(1, *z1)

        rows = out_2[0].bitcast(I32)
        view = osc[:].bitcast(I32)
        for q in range(4):
            queue = nc.scalar if q % 2 == 0 else nc.sync
            queue.dma_start(out=rows[4 * q : 4 * q + 4, :], in_=view[32 * q : 32 * q + 4, :])
